import numpy as np
import ml_dtypes


def mxq(x, axis, fmt="e4m3"):
    dtype, down = {"e4m3": (ml_dtypes.float8_e4m3fn, 7), "e5m2": (ml_dtypes.float8_e5m2, 14)}[fmt]
    v = np.moveaxis(np.asarray(x, np.float32).astype(ml_dtypes.bfloat16).astype(np.float64), axis, -1)
    blocks = v.reshape(v.shape[:-1] + (-1, 32))
    amax = np.abs(blocks).max(-1, keepdims=True)
    byte = np.maximum(np.where(amax > 0, np.frexp(amax)[1] - 1 + 127, 0) - down, 1)
    scale = np.exp2(byte - 127.0)
    codes = (blocks / scale).astype(np.float32).astype(dtype).astype(np.float64)
    return np.moveaxis((codes * scale).reshape(v.shape), -1, axis)


WIDE = False


def mx_kscale(k):
    if not WIDE:
        return np.ones(k)
    levels = np.array([10, -10, 5, -5, 0])
    if k % 512:
        return np.exp2(np.random.permutation(np.resize(levels, k // 32))).repeat(32)
    a = np.empty((k // 512, 16))
    for p in range(k // 512):
        a[p, :8] = np.random.permutation(np.resize(levels, 8))
        for g in range(8):
            far = levels[np.abs(levels - a[p, g]) >= 10]
            a[p, g + 8] = far[np.random.randint(len(far))]
    return np.exp2(a.ravel()).repeat(32)


def f64(x):
    return np.asarray(x).astype(np.float64)


E2M1 = np.array([0.0, 0.5, 1.0, 1.5, 2.0, 3.0, 4.0, 6.0, -0.0, -0.5, -1.0, -1.5, -2.0, -3.0, -4.0, -6.0])


def pack_weight(w, fmt):
    k, n = w.shape
    w = f64(np.asarray(w, np.float32).astype(ml_dtypes.bfloat16)).reshape(k // 32, 32, n)
    amax = np.abs(w).max(1)
    if fmt == "e4m3":
        byte = np.frexp(amax)[1] - 1 + 127 - 7
    else:
        mant, ex = np.frexp(amax / 6.0)
        byte = np.where(mant > 0.5, ex, ex - 1) + 127
    byte = np.clip(np.where(amax > 0, byte, 1), 1, 254)
    scaled = (w * np.exp2(127.0 - byte)[:, None, :]).reshape(k, n).astype(np.float32)
    by_word = np.ascontiguousarray(scaled.reshape(k // 512, 128, 4, n).transpose(0, 1, 3, 2))
    if fmt == "e4m3":
        words = by_word.astype(ml_dtypes.float8_e4m3fn).view(np.uint8)
    else:
        c = by_word.astype(ml_dtypes.float4_e2m1fn).view(np.uint8) & 0xF
        words = (c[..., 0::2] | (c[..., 1::2] << 4)).reshape(k // 512, 128, 2 * n)
    return np.ascontiguousarray(words), np.ascontiguousarray(byte.astype(np.uint8).reshape(k // 512, 16, n))


def unpack_weight(words, scales, fmt):
    g, _, n = scales.shape
    words = np.ascontiguousarray(words).reshape(g, 128, n, -1)
    if fmt == "e4m3":
        vals = words.view(ml_dtypes.float8_e4m3fn).astype(np.float64)
    else:
        nib = np.empty((g, 128, n, 4), np.uint8)
        nib[..., 0::2] = words & 0xF
        nib[..., 1::2] = words >> 4
        vals = E2M1[nib]
    vals = vals * np.repeat(np.exp2(scales.astype(np.float64) - 127.0), 8, axis=1)[..., None]
    return vals.transpose(0, 1, 3, 2).reshape(g * 512, n)


K, L, T, R, N = 1024, 512, 512, 512, 512


def setup_inputs():
    n = np.random.standard_normal
    fk = mx_kscale(K)
    fl = mx_kscale(L)
    fr = mx_kscale(R)
    xtp = pack_weight(n((K, T)) / fk[:, None], "e4m3")
    wap = pack_weight(n((K, R)) * 1.4 / np.sqrt(K) * fk[:, None], "e2m1")
    xqp = pack_weight(n((L, T)) / fl[:, None], "e4m3")
    wcp = pack_weight(n((L, R)) * 1 / np.sqrt(L) * fl[:, None], "e2m1")
    wbp = pack_weight(n((R, N)) * 1 / np.sqrt(R) / fr[:, None], "e4m3")
    wdp = pack_weight(n((R, N)) * 1 / np.sqrt(R) / fr[:, None], "e2m1")
    return {
        "xt_words": xtp[0],
        "xt_scales": xtp[1],
        "wa_words": wap[0],
        "wa_scales": wap[1],
        "xq_words": xqp[0],
        "xq_scales": xqp[1],
        "wc_words": wcp[0],
        "wc_scales": wcp[1],
        "us": (np.random.uniform(0.5, 2.0, (R, 1)) * fr[:, None]).astype(np.float32),
        "ur": (np.random.uniform(0.5, 2.0, (R, 1)) * fr[:, None]).astype(np.float32),
        "wb_words": wbp[0],
        "wb_scales": wbp[1],
        "wd_words": wdp[0],
        "wd_scales": wdp[1],
    }


def reference(xt_words, xt_scales, wa_words, wa_scales, xq_words, xq_scales, wc_words, wc_scales, us, ur, wb_words, wb_scales, wd_words, wd_scales):
    xtu = unpack_weight(xt_words, xt_scales, "e4m3")
    wau = unpack_weight(wa_words, wa_scales, "e2m1")
    xqu = unpack_weight(xq_words, xq_scales, "e4m3")
    wcu = unpack_weight(wc_words, wc_scales, "e2m1")
    wbu = unpack_weight(wb_words, wb_scales, "e4m3")
    wdu = unpack_weight(wd_words, wd_scales, "e2m1")
    z = wau.T @ xtu + wcu.T @ xqu
    kp = np.maximum(np.minimum(z, 1.0), 0.0 - 1.0)
    ha = kp * f64(us)
    hb = (z - kp) * f64(ur)
    haq = mxq(ha, 0, "e4m3")
    hbq = mxq(hb, 0, "e4m3")
    y = wbu.T @ haq + wdu.T @ hbq
    return y

@@ -1,0 +1,212 @@
+from contextlib import ExitStack
+
+import concourse.mybir as mybir
+from concourse.masks import make_identity
+
+K, L, T, R, N = 1024, 512, 512, 512, 512
+FLOPS = 2 * (K + L) * R * T + 2 * 2 * R * N * T
+
+F32 = mybir.dt.float32
+BF16 = mybir.dt.bfloat16
+I32 = mybir.dt.int32
+U32 = mybir.dt.uint32
+U16 = mybir.dt.uint16
+U8 = mybir.dt.uint8
+FP8X4 = mybir.dt.float8_e4m3fn_x4
+FP4X4 = mybir.dt.float4_e2m1fn_x4
+ALU = mybir.AluOpType
+
+P = 128
+PACK = 4
+TC = 128
+CHUNKS = T // TC
+PASSES = (K + L) // (P * PACK)
+
+
+def tile_mix_hidden_kept_and_cut_off_kernel(
+    tc, xt_words, xt_scales, wa_words, wa_scales, xq_words, xq_scales, wc_words, wc_scales,
+    us, ur, wb_words, wb_scales, wd_words, wd_scales, out,
+):
+    nc = tc.nc
+    with ExitStack() as ctx:
+        sb = ctx.enter_context(tc.tile_pool(name="sb", bufs=1))
+        ps = ctx.enter_context(tc.psum_pool(name="ps", bufs=1))
+        ctx.enter_context(tc.manual_schedule())
+
+        wa_raw = sb.tile([P, 2, 2 * R], U8, align_bytes=64)
+        wc_raw = sb.tile([P, 1, 2 * R], U8, align_bytes=64)
+        w1_scales_raw = sb.tile([P, PASSES * R], U8, align_bytes=64)
+        planes = sb.tile([P, 5 * 512], U8, align_bytes=64)
+        xt_codes = sb.tile([P, 2, T], U32, align_bytes=64)
+        xq_codes = sb.tile([P, 1, T], U32, align_bytes=64)
+        wb_codes = sb.tile([P, 1, N], U32, align_bytes=64)
+        wd_codes = sb.tile([P, 1, 2 * N], U8, align_bytes=64)
+        us_cols = sb.tile([P, PACK], F32)
+        ur_row = sb.tile([P, R], F32)
+        ident = sb.tile([P, P], F32)
+
+        nc.vector.memset(w1_scales_raw[:].bitcast(I32), 0)
+        nc.vector.memset(planes[:].bitcast(I32), 0)
+        nc.gpsimd.memset(ur_row[:], 0.0)
+        make_identity(nc, ident[:])
+
+        queues = [nc.sync, nc.scalar]
+
+        def load_words(queue, dst, words):
+            if words.ndim == 4:
+                words = words.rearrange("g p n t -> g p (n t)")
+            queue.dma_start(out=dst[:].bitcast(I32), in_=words.rearrange("g p b -> p g b").bitcast(I32))
+
+        def load_scales(dst, scales):
+            passes = scales.shape[0]
+            for q in range(4):
+                queues[q % 2].dma_start(
+                    out=dst[32 * q : 32 * q + 4, :].bitcast(I32).rearrange("r (g c) -> r g c", g=passes),
+                    in_=scales[:, 4 * q : 4 * q + 4, :].rearrange("g r c -> r g c").bitcast(I32),
+                )
+
+        load_words(nc.sync, wa_raw, wa_words)
+        load_words(nc.scalar, wc_raw, wc_words)
+        load_scales(w1_scales_raw[:, 0 : 2 * R], wa_scales)
+        load_words(nc.sync, xt_codes, xt_words)
+        load_scales(planes[:, 0:1024], xt_scales)
+        load_scales(w1_scales_raw[:, 2 * R : 3 * R], wc_scales)
+        load_words(nc.scalar, xq_codes, xq_words)
+        load_scales(planes[:, 1024:1536], xq_scales)
+        nc.sync.dma_start(out=ur_row[0:1, :], in_=ur.rearrange("r o -> o r"))
+        nc.scalar.dma_start(out=us_cols[:], in_=us.rearrange("(p j) o -> p (j o)", j=PACK))
+        load_words(nc.sync, wb_codes, wb_words)
+        load_words(nc.scalar, wd_codes, wd_words)
+        load_scales(planes[:, 1536:2048], wb_scales)
+        load_scales(planes[:, 2048:2560], wd_scales)
+
+        w1_raw = [wa_raw[:, 0, :], wa_raw[:, 1, :], wc_raw[:, 0, :]]
+        x_codes = [xt_codes[:, 0, :], xt_codes[:, 1, :], xq_codes[:, 0, :]]
+        w1_codes = []
+        w1_scales = []
+        for g in range(PASSES):
+            codes = sb.tile([P, 2 * R], U8, align_bytes=64, name="w1_codes%d" % g)
+            scales = sb.tile([P, R], U8, align_bytes=64, name="w1_scales%d" % g)
+            nc.vector.tensor_copy(
+                out=codes[:].bitcast(U16).rearrange("p (j m) -> p j m", j=PACK),
+                in_=w1_raw[g].bitcast(U16).rearrange("p (m j) -> p j m", j=PACK),
+            )
+            nc.vector.tensor_copy(
+                out=scales[:].rearrange("p (j m) -> p j m", j=PACK),
+                in_=w1_scales_raw[:, g * R : (g + 1) * R].rearrange("p (m j) -> p j m", j=PACK),
+            )
+            w1_codes.append(codes)
+            w1_scales.append(scales)
+
+        z = [ps.tile([P, PACK * TC], F32, name="z%d" % c, tag="bank", bufs=7) for c in range(CHUNKS)]
+        ur_bank = ps.tile([P, PACK, P], F32)
+
+        def first_layer(c, g):
+            for j in range(PACK):
+                nc.tensor.matmul_mx(
+                    out=z[c][:, j * TC : (j + 1) * TC],
+                    lhsT=w1_codes[g][:, 2 * P * j : 2 * P * (j + 1)].bitcast(FP4X4),
+                    lhsT_scale=w1_scales[g][:, P * j : P * (j + 1)],
+                    rhs=x_codes[g][:, c * TC : (c + 1) * TC].bitcast(FP8X4),
+                    rhs_scale=planes[:, g * T + c * TC : g * T + (c + 1) * TC],
+                    start=(g == 0 and j == 0),
+                    stop=(g == PASSES - 1 and j == PACK - 1),
+                )
+
+        for g in range(PASSES):
+            first_layer(0, g)
+            first_layer(1, g)
+        for j in range(PACK):
+            nc.tensor.transpose(ur_bank[:, j, :], ur_row[:, j:R:PACK], ident[:])
+        for c in range(2, CHUNKS):
+            for g in range(PASSES):
+                first_layer(c, g)
+
+        W = PACK * TC
+        kept = [sb.tile([P, W], F32, name="kept%d" % c) for c in range(CHUNKS)]
+        cut = [sb.tile([P, W], F32, name="cut%d" % c) for c in range(CHUNKS)]
+        hidden = [sb.tile([P, 2 * W], BF16, name="hidden%d" % c, align_bytes=64) for c in range(CHUNKS)]
+        h_codes = [sb.tile([P, 2 * TC], U32, name="h_codes%d" % c, align_bytes=64) for c in range(CHUNKS)]
+        h_scales = [sb.tile([P, 2 * TC], U8, name="h_scales%d" % c, align_bytes=64) for c in range(CHUNKS)]
+
+        def by_token(ap):
+            return ap.rearrange("p (t j) -> p t j", j=PACK)
+
+        def z_by_token(c):
+            return z[c][:].rearrange("p (j t) -> p t j", j=PACK)
+
+        us_b = us_cols[:].unsqueeze(1).to_broadcast([P, TC, PACK])
+        ur_b = ur_bank[:, :, 0].unsqueeze(1).to_broadcast([P, TC, PACK])
+
+        def keep(c):
+            nc.vector.tensor_scalar(
+                out=by_token(kept[c][:]), in0=z_by_token(c), scalar1=1.0, scalar2=-1.0, op0=ALU.min, op1=ALU.max
+            )
+            nc.gpsimd.tensor_tensor(out=by_token(hidden[c][:, 0:W]), in0=by_token(kept[c][:]), in1=us_b, op=ALU.mult)
+
+        def cut_off(c):
+            nc.vector.tensor_tensor(out=by_token(cut[c][:]), in0=z_by_token(c), in1=by_token(kept[c][:]), op=ALU.subtract)
+
+        def scale_cut(c):
+            nc.vector.tensor_tensor(out=by_token(hidden[c][:, W : 2 * W]), in0=by_token(cut[c][:]), in1=ur_b, op=ALU.mult)
+
+        def quantise(c, first, count):
+            nc.vector.quantize_mx(
+                out=h_codes[c][:, first * TC : (first + count) * TC].bitcast(FP8X4),
+                scales=h_scales[c][:, first * TC : (first + count) * TC],
+                in_=hidden[c][:, first * W : (first + count) * W],
+            )
+
+        out_v = out.rearrange("(i p) t -> p i t", p=P)
+
+        def second_layer(c, groups):
+            banks = [ps.tile([P, len(g) * TC], F32, name="y%d_%d" % (c, g[0]), tag="bank", bufs=7) for g in groups]
+            for part in range(2):
+                for bank, tiles in zip(banks, groups):
+                    for s, i in enumerate(tiles):
+                        if part == 0:
+                            lhsT = wb_codes[:, 0, P * i : P * (i + 1)].bitcast(FP8X4)
+                        else:
+                            lhsT = wd_codes[:, 0, 2 * P * i : 2 * P * (i + 1)].bitcast(FP4X4)
+                        nc.tensor.matmul_mx(
+                            out=bank[:, s * TC : (s + 1) * TC],
+                            lhsT=lhsT,
+                            lhsT_scale=planes[:, (3 + part) * 512 + P * i : (3 + part) * 512 + P * (i + 1)],
+                            rhs=h_codes[c][:, part * TC : (part + 1) * TC].bitcast(FP8X4),
+                            rhs_scale=h_scales[c][:, part * TC : (part + 1) * TC],
+                            start=(part == 0 and s == 0),
+                            stop=(part == 1 and s == len(tiles) - 1),
+                        )
+            for b, (bank, tiles) in enumerate(zip(banks, groups)):
+                res = sb.tile([P, len(tiles) * TC], F32, name="res%d_%d" % (c, b))
+                if b == 0:
+                    nc.scalar.copy(out=res[:], in_=bank[:])
+                else:
+                    nc.vector.tensor_copy(out=res[:], in_=bank[:])
+                queues[b].dma_start(
+                    out=out_v[:, tiles[0] : tiles[-1] + 1, c * TC : (c + 1) * TC],
+                    in_=res[:].rearrange("p (i t) -> p i t", t=TC),
+                )
+
+        whole = [[0, 1, 2, 3]]
+        keep(0)
+        keep(1)
+        cut_off(0)
+        cut_off(1)
+        scale_cut(0)
+        keep(2)
+        quantise(0, 0, 2)
+        second_layer(0, whole)
+        scale_cut(1)
+        cut_off(2)
+        quantise(1, 0, 2)
+        second_layer(1, whole)
+        keep(3)
+        scale_cut(2)
+        cut_off(3)
+        quantise(2, 0, 2)
+        second_layer(2, whole)
+        scale_cut(3)
+        quantise(3, 0, 1)
+        quantise(3, 1, 1)
+        second_layer(3, [[0, 1], [2, 3]])

@@ -35,53 +35,63 @@ def tile_mix_hidden_kept_and_cut_off_kernel(
 
         wa_raw = sb.tile([P, 2, 2 * R], U8, align_bytes=64)
         wc_raw = sb.tile([P, 1, 2 * R], U8, align_bytes=64)
-        w1_scales_raw = sb.tile([P, PASSES * R], U8, align_bytes=64)
-        planes = sb.tile([P, 5 * 512], U8, align_bytes=64)
+        wa_plane = sb.tile([P, 2 * R], U8, align_bytes=64)
+        wc_plane = sb.tile([P, R], U8, align_bytes=64)
+        xt_plane = sb.tile([P, 2 * T], U8, align_bytes=64)
+        xq_plane = sb.tile([P, T], U8, align_bytes=64)
+        wb_plane = sb.tile([P, N], U8, align_bytes=64)
+        wd_plane = sb.tile([P, N], U8, align_bytes=64)
         xt_codes = sb.tile([P, 2, T], U32, align_bytes=64)
         xq_codes = sb.tile([P, 1, T], U32, align_bytes=64)
         wb_codes = sb.tile([P, 1, N], U32, align_bytes=64)
         wd_codes = sb.tile([P, 1, 2 * N], U8, align_bytes=64)
         us_cols = sb.tile([P, PACK], F32)
-        ur_row = sb.tile([P, R], F32)
+        ur_row = sb.tile([1, R], F32)
+        ur_slots = sb.tile([P, R], F32)
         ident = sb.tile([P, P], F32)
 
-        nc.vector.memset(w1_scales_raw[:].bitcast(I32), 0)
-        nc.vector.memset(planes[:].bitcast(I32), 0)
-        nc.gpsimd.memset(ur_row[:], 0.0)
-        make_identity(nc, ident[:])
+        nc.gpsimd.memset(xt_plane[:].bitcast(I32), 0)
+        nc.vector.memset(wa_plane[:].bitcast(I32), 0)
+        nc.vector.memset(xq_plane[:].bitcast(I32), 0)
+        nc.vector.memset(wc_plane[:].bitcast(I32), 0)
 
-        queues = [nc.sync, nc.scalar]
+        both = [nc.sync, nc.scalar]
 
         def load_words(queue, dst, words):
             if words.ndim == 4:
                 words = words.rearrange("g p n t -> g p (n t)")
             queue.dma_start(out=dst[:].bitcast(I32), in_=words.rearrange("g p b -> p g b").bitcast(I32))
 
-        def load_scales(dst, scales):
+        def load_scales(queues, dst, scales, quadrants):
             passes = scales.shape[0]
-            for q in range(4):
-                queues[q % 2].dma_start(
+            for q in quadrants:
+                queues[q % len(queues)].dma_start(
                     out=dst[32 * q : 32 * q + 4, :].bitcast(I32).rearrange("r (g c) -> r g c", g=passes),
                     in_=scales[:, 4 * q : 4 * q + 4, :].rearrange("g r c -> r g c").bitcast(I32),
                 )
 
+        load_scales([nc.gpsimd], xt_plane, xt_scales, range(2))
+        load_scales([nc.gpsimd], xq_plane, xq_scales, range(2))
+
+        swapped = [nc.scalar, nc.sync]
         load_words(nc.sync, wa_raw, wa_words)
-        load_words(nc.scalar, wc_raw, wc_words)
-        load_scales(w1_scales_raw[:, 0 : 2 * R], wa_scales)
-        load_words(nc.sync, xt_codes, xt_words)
-        load_scales(planes[:, 0:1024], xt_scales)
-        load_scales(w1_scales_raw[:, 2 * R : 3 * R], wc_scales)
+        load_scales(swapped, wa_plane, wa_scales, range(4))
+        load_scales(swapped, xt_plane, xt_scales, range(2, 4))
+        load_words(nc.scalar, xt_codes, xt_words)
+        load_words(nc.sync, wc_raw, wc_words)
         load_words(nc.scalar, xq_codes, xq_words)
-        load_scales(planes[:, 1024:1536], xq_scales)
-        nc.sync.dma_start(out=ur_row[0:1, :], in_=ur.rearrange("r o -> o r"))
-        nc.scalar.dma_start(out=us_cols[:], in_=us.rearrange("(p j) o -> p (j o)", j=PACK))
+        load_scales(both, wc_plane, wc_scales, range(4))
+        load_scales(both, xq_plane, xq_scales, range(2, 4))
+        nc.sync.dma_start(out=ur_row[:], in_=ur.rearrange("r o -> o r"))
+        nc.sync.dma_start(out=us_cols[:], in_=us.rearrange("(p j) o -> p (j o)", j=PACK))
         load_words(nc.sync, wb_codes, wb_words)
-        load_words(nc.scalar, wd_codes, wd_words)
-        load_scales(planes[:, 1536:2048], wb_scales)
-        load_scales(planes[:, 2048:2560], wd_scales)
+        load_words(nc.sync, wd_codes, wd_words)
 
         w1_raw = [wa_raw[:, 0, :], wa_raw[:, 1, :], wc_raw[:, 0, :]]
         x_codes = [xt_codes[:, 0, :], xt_codes[:, 1, :], xq_codes[:, 0, :]]
+        x_planes = [xt_plane[:, 0:T], xt_plane[:, T : 2 * T], xq_plane[:]]
+        w1_planes = [wa_plane[:, 0:R], wa_plane[:, R : 2 * R], wc_plane[:]]
+        w2_planes = [wb_plane, wd_plane]
         w1_codes = []
         w1_scales = []
         for g in range(PASSES):
@@ -93,10 +103,18 @@ def tile_mix_hidden_kept_and_cut_off_kernel(
             )
             nc.vector.tensor_copy(
                 out=scales[:].rearrange("p (j m) -> p j m", j=PACK),
-                in_=w1_scales_raw[:, g * R : (g + 1) * R].rearrange("p (m j) -> p j m", j=PACK),
+                in_=w1_planes[g].rearrange("p (m j) -> p j m", j=PACK),
             )
             w1_codes.append(codes)
             w1_scales.append(scales)
+
+        nc.vector.memset(wb_plane[:].bitcast(I32), 0)
+        nc.vector.memset(wd_plane[:].bitcast(I32), 0)
+        nc.vector.memset(ur_slots[:], 0.0)
+        nc.vector.memset(ident[:], 0.0)
+        make_identity(nc, ident[:], nomemset=True)
+        load_scales([nc.sync], wb_plane, wb_scales, range(4))
+        load_scales([nc.sync], wd_plane, wd_scales, range(4))
 
         z = [ps.tile([P, PACK * TC], F32, name="z%d" % c, tag="bank", bufs=7) for c in range(CHUNKS)]
         ur_bank = ps.tile([P, PACK, P], F32)
@@ -108,26 +126,40 @@ def tile_mix_hidden_kept_and_cut_off_kernel(
                     lhsT=w1_codes[g][:, 2 * P * j : 2 * P * (j + 1)].bitcast(FP4X4),
                     lhsT_scale=w1_scales[g][:, P * j : P * (j + 1)],
                     rhs=x_codes[g][:, c * TC : (c + 1) * TC].bitcast(FP8X4),
-                    rhs_scale=planes[:, g * T + c * TC : g * T + (c + 1) * TC],
+                    rhs_scale=x_planes[g][:, c * TC : (c + 1) * TC],
                     start=(g == 0 and j == 0),
                     stop=(g == PASSES - 1 and j == PACK - 1),
                 )
 
-        for g in range(PASSES):
-            first_layer(0, g)
-            first_layer(1, g)
-        for j in range(PACK):
-            nc.tensor.transpose(ur_bank[:, j, :], ur_row[:, j:R:PACK], ident[:])
-        for c in range(2, CHUNKS):
+        def first_layer_chunk(c):
             for g in range(PASSES):
                 first_layer(c, g)
+
+        def spread_ur():
+            nc.vector.tensor_copy(
+                out=ur_slots[0:1, :].rearrange("o (j p) -> o j p", j=PACK),
+                in_=ur_row[:].rearrange("o (p j) -> o j p", j=PACK),
+            )
+            for j in range(PACK):
+                nc.tensor.transpose(ur_bank[:, j, :], ur_slots[:, j * P : (j + 1) * P], ident[:])
 
         W = PACK * TC
         kept = [sb.tile([P, W], F32, name="kept%d" % c) for c in range(CHUNKS)]
         cut = [sb.tile([P, W], F32, name="cut%d" % c) for c in range(CHUNKS)]
-        hidden = [sb.tile([P, 2 * W], BF16, name="hidden%d" % c, align_bytes=64) for c in range(CHUNKS)]
-        h_codes = [sb.tile([P, 2 * TC], U32, name="h_codes%d" % c, align_bytes=64) for c in range(CHUNKS)]
-        h_scales = [sb.tile([P, 2 * TC], U8, name="h_scales%d" % c, align_bytes=64) for c in range(CHUNKS)]
+        batches = [[(0, 0), (1, 0)], [(0, 1), (1, 1)], [(0, 2), (0, 3)], [(1, 2)], [(1, 3)]]
+        hidden = {}
+        h_codes = {}
+        h_scales = {}
+        batch_tiles = []
+        for b, batch in enumerate(batches):
+            values = sb.tile([P, len(batch) * W], BF16, name="hidden%d" % b, align_bytes=64)
+            codes = sb.tile([P, len(batch) * TC], U32, name="h_codes%d" % b, align_bytes=64)
+            scales = sb.tile([P, len(batch) * TC], U8, name="h_scales%d" % b, align_bytes=64)
+            batch_tiles.append((values, codes, scales))
+            for s, key in enumerate(batch):
+                hidden[key] = values[:, s * W : (s + 1) * W]
+                h_codes[key] = codes[:, s * TC : (s + 1) * TC]
+                h_scales[key] = scales[:, s * TC : (s + 1) * TC]
 
         def by_token(ap):
             return ap.rearrange("p (t j) -> p t j", j=PACK)
@@ -142,42 +174,42 @@ def tile_mix_hidden_kept_and_cut_off_kernel(
             nc.vector.tensor_scalar(
                 out=by_token(kept[c][:]), in0=z_by_token(c), scalar1=1.0, scalar2=-1.0, op0=ALU.min, op1=ALU.max
             )
-            nc.gpsimd.tensor_tensor(out=by_token(hidden[c][:, 0:W]), in0=by_token(kept[c][:]), in1=us_b, op=ALU.mult)
+            nc.gpsimd.tensor_tensor(out=by_token(hidden[0, c]), in0=by_token(kept[c][:]), in1=us_b, op=ALU.mult)
 
         def cut_off(c):
             nc.vector.tensor_tensor(out=by_token(cut[c][:]), in0=z_by_token(c), in1=by_token(kept[c][:]), op=ALU.subtract)
 
         def scale_cut(c):
-            nc.vector.tensor_tensor(out=by_token(hidden[c][:, W : 2 * W]), in0=by_token(cut[c][:]), in1=ur_b, op=ALU.mult)
+            nc.vector.tensor_tensor(out=by_token(hidden[1, c]), in0=by_token(cut[c][:]), in1=ur_b, op=ALU.mult)
 
-        def quantise(c, first, count):
-            nc.vector.quantize_mx(
-                out=h_codes[c][:, first * TC : (first + count) * TC].bitcast(FP8X4),
-                scales=h_scales[c][:, first * TC : (first + count) * TC],
-                in_=hidden[c][:, first * W : (first + count) * W],
-            )
+        def quantise(b):
+            values, codes, scales = batch_tiles[b]
+            nc.vector.quantize_mx(out=codes[:].bitcast(FP8X4), scales=scales[:], in_=values[:])
 
         out_v = out.rearrange("(i p) t -> p i t", p=P)
 
-        def second_layer(c, groups):
-            banks = [ps.tile([P, len(g) * TC], F32, name="y%d_%d" % (c, g[0]), tag="bank", bufs=7) for g in groups]
-            for part in range(2):
-                for bank, tiles in zip(banks, groups):
-                    for s, i in enumerate(tiles):
-                        if part == 0:
-                            lhsT = wb_codes[:, 0, P * i : P * (i + 1)].bitcast(FP8X4)
-                        else:
-                            lhsT = wd_codes[:, 0, 2 * P * i : 2 * P * (i + 1)].bitcast(FP4X4)
-                        nc.tensor.matmul_mx(
-                            out=bank[:, s * TC : (s + 1) * TC],
-                            lhsT=lhsT,
-                            lhsT_scale=planes[:, (3 + part) * 512 + P * i : (3 + part) * 512 + P * (i + 1)],
-                            rhs=h_codes[c][:, part * TC : (part + 1) * TC].bitcast(FP8X4),
-                            rhs_scale=h_scales[c][:, part * TC : (part + 1) * TC],
-                            start=(part == 0 and s == 0),
-                            stop=(part == 1 and s == len(tiles) - 1),
-                        )
-            for b, (bank, tiles) in enumerate(zip(banks, groups)):
+        def open_banks(c, groups):
+            return [(ps.tile([P, len(g) * TC], F32, name="y%d_%d" % (c, g[0]), tag="bank", bufs=7), g) for g in groups]
+
+        def second_layer(part, c, banks):
+            for bank, tiles in banks:
+                for s, i in enumerate(tiles):
+                    if part == 0:
+                        lhsT = wb_codes[:, 0, P * i : P * (i + 1)].bitcast(FP8X4)
+                    else:
+                        lhsT = wd_codes[:, 0, 2 * P * i : 2 * P * (i + 1)].bitcast(FP4X4)
+                    nc.tensor.matmul_mx(
+                        out=bank[:, s * TC : (s + 1) * TC],
+                        lhsT=lhsT,
+                        lhsT_scale=w2_planes[part][:, P * i : P * (i + 1)],
+                        rhs=h_codes[part, c].bitcast(FP8X4),
+                        rhs_scale=h_scales[part, c],
+                        start=(part == 0 and s == 0),
+                        stop=(part == 1 and s == len(tiles) - 1),
+                    )
+
+        def store(c, banks, queues):
+            for b, (bank, tiles) in enumerate(banks):
                 res = sb.tile([P, len(tiles) * TC], F32, name="res%d_%d" % (c, b))
                 if b == 0:
                     nc.scalar.copy(out=res[:], in_=bank[:])
@@ -188,25 +220,40 @@ def tile_mix_hidden_kept_and_cut_off_kernel(
                     in_=res[:].rearrange("p (i t) -> p i t", t=TC),
                 )
 
-        whole = [[0, 1, 2, 3]]
+        def finish(c):
+            quantise(c)
+            banks = open_banks(c, [[0, 1, 2, 3]])
+            second_layer(0, c, banks)
+            second_layer(1, c, banks)
+            store(c, banks, [nc.sync])
+
+        first_layer_chunk(0)
+        first_layer_chunk(1)
         keep(0)
-        keep(1)
+        spread_ur()
+        first_layer_chunk(2)
+        first_layer_chunk(3)
         cut_off(0)
-        cut_off(1)
+        keep(1)
         scale_cut(0)
+        cut_off(1)
         keep(2)
-        quantise(0, 0, 2)
-        second_layer(0, whole)
+        finish(0)
         scale_cut(1)
-        cut_off(2)
-        quantise(1, 0, 2)
-        second_layer(1, whole)
         keep(3)
-        scale_cut(2)
+        finish(1)
+        cut_off(2)
         cut_off(3)
-        quantise(2, 0, 2)
-        second_layer(2, whole)
+        scale_cut(2)
+        quantise(2)
+        quantise(3)
+        banks2 = open_banks(2, [[0, 1, 2, 3]])
+        banks3 = open_banks(3, [[0, 1], [2, 3]])
+        second_layer(0, 2, banks2)
+        second_layer(1, 2, banks2)
+        second_layer(0, 3, banks3)
+        store(2, banks2, [nc.sync])
         scale_cut(3)
-        quantise(3, 0, 1)
-        quantise(3, 1, 1)
-        second_layer(3, [[0, 1], [2, 3]])
+        quantise(4)
+        second_layer(1, 3, banks3)
+        store(3, banks3, [nc.scalar, nc.sync])

@@ -15,12 +15,14 @@ U8 = mybir.dt.uint8
 FP8X4 = mybir.dt.float8_e4m3fn_x4
 FP4X4 = mybir.dt.float4_e2m1fn_x4
 ALU = mybir.AluOpType
+COPY = mybir.ActivationFunctionType.Copy
 
 P = 128
 PACK = 4
 TC = 128
 CHUNKS = T // TC
 PASSES = (K + L) // (P * PACK)
+SCALAR_TOKENS = 64
 
 
 def tile_mix_hidden_kept_and_cut_off_kernel(
@@ -41,8 +43,10 @@ def tile_mix_hidden_kept_and_cut_off_kernel(
         xq_plane = sb.tile([P, T], U8, align_bytes=64)
         wb_plane = sb.tile([P, N], U8, align_bytes=64)
         wd_plane = sb.tile([P, N], U8, align_bytes=64)
-        xt_codes = sb.tile([P, 2, T], U32, align_bytes=64)
-        xq_codes = sb.tile([P, 1, T], U32, align_bytes=64)
+        HALF = T // 2
+        xt_codes = [sb.tile([P, 2, HALF], U32, name="xt_codes%d" % h, align_bytes=64) for h in range(2)]
+        xq_codes = [sb.tile([P, 1, HALF], U32, name="xq_codes%d" % h, align_bytes=64) for h in range(2)]
+        ur_cols = sb.tile([P, PACK], F32)
         wb_codes = sb.tile([P, 1, N], U32, align_bytes=64)
         wd_codes = sb.tile([P, 1, 2 * N], U8, align_bytes=64)
         us_cols = sb.tile([P, PACK], F32)
@@ -72,23 +76,26 @@ def tile_mix_hidden_kept_and_cut_off_kernel(
 
         load_scales([nc.gpsimd], xt_plane, xt_scales, range(2))
         load_scales([nc.gpsimd], xq_plane, xq_scales, range(2))
+        make_identity(nc, ident[:])
 
         swapped = [nc.scalar, nc.sync]
         load_words(nc.sync, wa_raw, wa_words)
         load_scales(swapped, wa_plane, wa_scales, range(4))
         load_scales(swapped, xt_plane, xt_scales, range(2, 4))
-        load_words(nc.scalar, xt_codes, xt_words)
+        load_words(nc.scalar, xt_codes[0], xt_words[:, :, 0:HALF, :])
         load_words(nc.sync, wc_raw, wc_words)
-        load_words(nc.scalar, xq_codes, xq_words)
+        load_words(nc.scalar, xq_codes[0], xq_words[:, :, 0:HALF, :])
         load_scales(both, wc_plane, wc_scales, range(4))
         load_scales(both, xq_plane, xq_scales, range(2, 4))
         nc.sync.dma_start(out=ur_row[:], in_=ur.rearrange("r o -> o r"))
         nc.sync.dma_start(out=us_cols[:], in_=us.rearrange("(p j) o -> p (j o)", j=PACK))
+        load_words(nc.sync, xt_codes[1], xt_words[:, :, HALF:T, :])
+        load_words(nc.sync, xq_codes[1], xq_words[:, :, HALF:T, :])
         load_words(nc.sync, wb_codes, wb_words)
         load_words(nc.sync, wd_codes, wd_words)
 
         w1_raw = [wa_raw[:, 0, :], wa_raw[:, 1, :], wc_raw[:, 0, :]]
-        x_codes = [xt_codes[:, 0, :], xt_codes[:, 1, :], xq_codes[:, 0, :]]
+        x_codes = [[xt_codes[h][:, 0, :], xt_codes[h][:, 1, :], xq_codes[h][:, 0, :]] for h in range(2)]
         x_planes = [xt_plane[:, 0:T], xt_plane[:, T : 2 * T], xq_plane[:]]
         w1_planes = [wa_plane[:, 0:R], wa_plane[:, R : 2 * R], wc_plane[:]]
         w2_planes = [wb_plane, wd_plane]
@@ -110,11 +117,15 @@ def tile_mix_hidden_kept_and_cut_off_kernel(
 
         nc.vector.memset(wb_plane[:].bitcast(I32), 0)
         nc.vector.memset(wd_plane[:].bitcast(I32), 0)
-        nc.vector.memset(ur_slots[:], 0.0)
-        nc.vector.memset(ident[:], 0.0)
-        make_identity(nc, ident[:], nomemset=True)
         load_scales([nc.sync], wb_plane, wb_scales, range(4))
         load_scales([nc.sync], wd_plane, wd_scales, range(4))
+
+        nc.scalar.activation(
+            out=ur_slots[:].rearrange("p (j m) -> p j m", j=PACK),
+            in_=ident[:].unsqueeze(1).to_broadcast([P, PACK, P]),
+            func=COPY,
+            scale=0.0,
+        )
 
         z = [ps.tile([P, PACK * TC], F32, name="z%d" % c, tag="bank", bufs=7) for c in range(CHUNKS)]
         ur_bank = ps.tile([P, PACK, P], F32)
@@ -125,7 +136,7 @@ def tile_mix_hidden_kept_and_cut_off_kernel(
                     out=z[c][:, j * TC : (j + 1) * TC],
                     lhsT=w1_codes[g][:, 2 * P * j : 2 * P * (j + 1)].bitcast(FP4X4),
                     lhsT_scale=w1_scales[g][:, P * j : P * (j + 1)],
-                    rhs=x_codes[g][:, c * TC : (c + 1) * TC].bitcast(FP8X4),
+                    rhs=x_codes[c // 2][g][:, c % 2 * TC : (c % 2 + 1) * TC].bitcast(FP8X4),
                     rhs_scale=x_planes[g][:, c * TC : (c + 1) * TC],
                     start=(g == 0 and j == 0),
                     stop=(g == PASSES - 1 and j == PACK - 1),
@@ -136,17 +147,18 @@ def tile_mix_hidden_kept_and_cut_off_kernel(
                 first_layer(c, g)
 
         def spread_ur():
-            nc.vector.tensor_copy(
+            nc.scalar.copy(
                 out=ur_slots[0:1, :].rearrange("o (j p) -> o j p", j=PACK),
                 in_=ur_row[:].rearrange("o (p j) -> o j p", j=PACK),
             )
             for j in range(PACK):
                 nc.tensor.transpose(ur_bank[:, j, :], ur_slots[:, j * P : (j + 1) * P], ident[:])
+            nc.scalar.copy(out=ur_cols[:], in_=ur_bank[:, :, 0])
 
         W = PACK * TC
         kept = [sb.tile([P, W], F32, name="kept%d" % c) for c in range(CHUNKS)]
         cut = [sb.tile([P, W], F32, name="cut%d" % c) for c in range(CHUNKS)]
-        batches = [[(0, 0), (1, 0)], [(0, 1), (1, 1)], [(0, 2), (0, 3)], [(1, 2)], [(1, 3)]]
+        batches = [[(0, c), (1, c)] for c in range(CHUNKS)]
         hidden = {}
         h_codes = {}
         h_scales = {}
@@ -168,7 +180,6 @@ def tile_mix_hidden_kept_and_cut_off_kernel(
             return z[c][:].rearrange("p (j t) -> p t j", j=PACK)
 
         us_b = us_cols[:].unsqueeze(1).to_broadcast([P, TC, PACK])
-        ur_b = ur_bank[:, :, 0].unsqueeze(1).to_broadcast([P, TC, PACK])
 
         def keep(c):
             nc.vector.tensor_scalar(
@@ -179,8 +190,22 @@ def tile_mix_hidden_kept_and_cut_off_kernel(
         def cut_off(c):
             nc.vector.tensor_tensor(out=by_token(cut[c][:]), in0=z_by_token(c), in1=by_token(kept[c][:]), op=ALU.subtract)
 
-        def scale_cut(c):
-            nc.vector.tensor_tensor(out=by_token(hidden[1, c]), in0=by_token(cut[c][:]), in1=ur_b, op=ALU.mult)
+        def scale_cut(c, first):
+            nc.vector.tensor_tensor(
+                out=by_token(hidden[1, c])[:, first:TC, :],
+                in0=by_token(cut[c][:])[:, first:TC, :],
+                in1=ur_bank[:, :, 0].unsqueeze(1).to_broadcast([P, TC - first, PACK]),
+                op=ALU.mult,
+            )
+
+        def scale_cut_on_scalar(c):
+            for j in range(PACK):
+                nc.scalar.activation(
+                    out=by_token(hidden[1, c])[:, 0:SCALAR_TOKENS, j],
+                    in_=by_token(cut[c][:])[:, 0:SCALAR_TOKENS, j],
+                    func=COPY,
+                    scale=ur_cols[:, j : j + 1],
+                )
 
         def quantise(b):
             values, codes, scales = batch_tiles[b]
@@ -220,13 +245,14 @@ def tile_mix_hidden_kept_and_cut_off_kernel(
                     in_=res[:].rearrange("p (i t) -> p i t", t=TC),
                 )
 
-        def finish(c):
+        def multiply(c, groups):
             quantise(c)
-            banks = open_banks(c, [[0, 1, 2, 3]])
+            banks = open_banks(c, groups)
             second_layer(0, c, banks)
             second_layer(1, c, banks)
-            store(c, banks, [nc.sync])
+            return banks
 
+        whole = [[0, 1, 2, 3]]
         first_layer_chunk(0)
         first_layer_chunk(1)
         keep(0)
@@ -234,26 +260,22 @@ def tile_mix_hidden_kept_and_cut_off_kernel(
         first_layer_chunk(2)
         first_layer_chunk(3)
         cut_off(0)
+        scale_cut_on_scalar(0)
         keep(1)
-        scale_cut(0)
+        scale_cut(0, SCALAR_TOKENS)
         cut_off(1)
+        scale_cut_on_scalar(1)
         keep(2)
-        finish(0)
-        scale_cut(1)
-        keep(3)
-        finish(1)
+        store(0, multiply(0, whole), [nc.sync])
+        scale_cut(1, SCALAR_TOKENS)
         cut_off(2)
+        scale_cut_on_scalar(2)
+        keep(3)
+        store(1, multiply(1, whole), [nc.sync])
         cut_off(3)
-        scale_cut(2)
-        quantise(2)
-        quantise(3)
-        banks2 = open_banks(2, [[0, 1, 2, 3]])
-        banks3 = open_banks(3, [[0, 1], [2, 3]])
-        second_layer(0, 2, banks2)
-        second_layer(1, 2, banks2)
-        second_layer(0, 3, banks3)
+        scale_cut(2, SCALAR_TOKENS)
+        scale_cut(3, 0)
+        banks2 = multiply(2, whole)
+        banks3 = multiply(3, [[0, 1], [2, 3]])
         store(2, banks2, [nc.sync])
-        scale_cut(3)
-        quantise(4)
-        second_layer(1, 3, banks3)
         store(3, banks3, [nc.scalar, nc.sync])

@@ -158,7 +158,7 @@ def tile_mix_hidden_kept_and_cut_off_kernel(
         W = PACK * TC
         kept = [sb.tile([P, W], F32, name="kept%d" % c) for c in range(CHUNKS)]
         cut = [sb.tile([P, W], F32, name="cut%d" % c) for c in range(CHUNKS)]
-        batches = [[(0, c), (1, c)] for c in range(CHUNKS)]
+        batches = [[(0, c), (1, c)] for c in range(CHUNKS - 1)] + [[(0, CHUNKS - 1)], [(1, CHUNKS - 1)]]
         hidden = {}
         h_codes = {}
         h_scales = {}
@@ -179,13 +179,17 @@ def tile_mix_hidden_kept_and_cut_off_kernel(
         def z_by_token(c):
             return z[c][:].rearrange("p (j t) -> p t j", j=PACK)
 
-        us_b = us_cols[:].unsqueeze(1).to_broadcast([P, TC, PACK])
 
-        def keep(c):
+        def keep(c, first):
             nc.vector.tensor_scalar(
                 out=by_token(kept[c][:]), in0=z_by_token(c), scalar1=1.0, scalar2=-1.0, op0=ALU.min, op1=ALU.max
             )
-            nc.gpsimd.tensor_tensor(out=by_token(hidden[0, c]), in0=by_token(kept[c][:]), in1=us_b, op=ALU.mult)
+            nc.gpsimd.tensor_tensor(
+                out=by_token(hidden[0, c])[:, first:TC, :],
+                in0=by_token(kept[c][:])[:, first:TC, :],
+                in1=us_cols[:].unsqueeze(1).to_broadcast([P, TC - first, PACK]),
+                op=ALU.mult,
+            )
 
         def cut_off(c):
             nc.vector.tensor_tensor(out=by_token(cut[c][:]), in0=z_by_token(c), in1=by_token(kept[c][:]), op=ALU.subtract)
@@ -198,13 +202,13 @@ def tile_mix_hidden_kept_and_cut_off_kernel(
                 op=ALU.mult,
             )
 
-        def scale_cut_on_scalar(c):
+        def scale_on_scalar(dst, src, factors):
             for j in range(PACK):
                 nc.scalar.activation(
-                    out=by_token(hidden[1, c])[:, 0:SCALAR_TOKENS, j],
-                    in_=by_token(cut[c][:])[:, 0:SCALAR_TOKENS, j],
+                    out=by_token(dst)[:, 0:SCALAR_TOKENS, j],
+                    in_=by_token(src[:])[:, 0:SCALAR_TOKENS, j],
                     func=COPY,
-                    scale=ur_cols[:, j : j + 1],
+                    scale=factors[:, j : j + 1],
                 )
 
         def quantise(b):
@@ -245,37 +249,44 @@ def tile_mix_hidden_kept_and_cut_off_kernel(
                     in_=res[:].rearrange("p (i t) -> p i t", t=TC),
                 )
 
-        def multiply(c, groups):
+        def multiply(c):
             quantise(c)
-            banks = open_banks(c, groups)
+            banks = open_banks(c, [[0, 1, 2, 3]])
             second_layer(0, c, banks)
             second_layer(1, c, banks)
             return banks
 
-        whole = [[0, 1, 2, 3]]
-        first_layer_chunk(0)
-        first_layer_chunk(1)
-        keep(0)
+        first_layer(0, 0)
+        first_layer(0, 1)
+        first_layer(1, 0)
+        first_layer(0, 2)
+        first_layer(1, 1)
+        first_layer(1, 2)
+        keep(0, 0)
         spread_ur()
         first_layer_chunk(2)
         first_layer_chunk(3)
         cut_off(0)
-        scale_cut_on_scalar(0)
-        keep(1)
+        scale_on_scalar(hidden[1, 0], cut[0], ur_cols)
+        keep(1, 0)
         scale_cut(0, SCALAR_TOKENS)
         cut_off(1)
-        scale_cut_on_scalar(1)
-        keep(2)
-        store(0, multiply(0, whole), [nc.sync])
+        scale_on_scalar(hidden[1, 1], cut[1], ur_cols)
+        keep(2, 0)
+        store(0, multiply(0), [nc.sync])
         scale_cut(1, SCALAR_TOKENS)
         cut_off(2)
-        scale_cut_on_scalar(2)
-        keep(3)
-        store(1, multiply(1, whole), [nc.sync])
-        cut_off(3)
+        scale_on_scalar(hidden[1, 2], cut[2], ur_cols)
+        keep(3, SCALAR_TOKENS)
+        scale_on_scalar(hidden[0, 3], kept[3], us_cols)
+        store(1, multiply(1), [nc.sync])
         scale_cut(2, SCALAR_TOKENS)
+        cut_off(3)
+        store(2, multiply(2), [nc.sync])
         scale_cut(3, 0)
-        banks2 = multiply(2, whole)
-        banks3 = multiply(3, [[0, 1], [2, 3]])
-        store(2, banks2, [nc.sync])
-        store(3, banks3, [nc.scalar, nc.sync])
+        quantise(3)
+        quantise(4)
+        banks = open_banks(3, [[0, 1], [2, 3]])
+        second_layer(0, 3, banks)
+        second_layer(1, 3, banks)
+        store(3, banks, [nc.scalar, nc.sync])

@@ -276,11 +276,10 @@ def tile_mix_hidden_kept_and_cut_off_kernel(
         store(0, multiply(0), [nc.sync])
         scale_cut(1, SCALAR_TOKENS)
         cut_off(2)
-        scale_on_scalar(hidden[1, 2], cut[2], ur_cols)
         keep(3, SCALAR_TOKENS)
         scale_on_scalar(hidden[0, 3], kept[3], us_cols)
         store(1, multiply(1), [nc.sync])
-        scale_cut(2, SCALAR_TOKENS)
+        scale_cut(2, 0)
         cut_off(3)
         store(2, multiply(2), [nc.sync])
         scale_cut(3, 0)

from contextlib import ExitStack

import concourse.mybir as mybir
from concourse.masks import make_identity

K, L, T, R, N = 1024, 512, 512, 512, 512
FLOPS = 2 * (K + L) * R * T + 2 * 2 * R * N * T

F32 = mybir.dt.float32
BF16 = mybir.dt.bfloat16
I32 = mybir.dt.int32
U32 = mybir.dt.uint32
U16 = mybir.dt.uint16
U8 = mybir.dt.uint8
FP8X4 = mybir.dt.float8_e4m3fn_x4
FP4X4 = mybir.dt.float4_e2m1fn_x4
ALU = mybir.AluOpType
COPY = mybir.ActivationFunctionType.Copy

P = 128
PACK = 4
TC = 128
CHUNKS = T // TC
PASSES = (K + L) // (P * PACK)
SCALAR_TOKENS = 64


def tile_mix_hidden_kept_and_cut_off_kernel(
    tc, xt_words, xt_scales, wa_words, wa_scales, xq_words, xq_scales, wc_words, wc_scales,
    us, ur, wb_words, wb_scales, wd_words, wd_scales, out,
):
    nc = tc.nc
    with ExitStack() as ctx:
        sb = ctx.enter_context(tc.tile_pool(name="sb", bufs=1))
        ps = ctx.enter_context(tc.psum_pool(name="ps", bufs=1))
        ctx.enter_context(tc.manual_schedule())

        wa_raw = sb.tile([P, 2, 2 * R], U8, align_bytes=64)
        wc_raw = sb.tile([P, 1, 2 * R], U8, align_bytes=64)
        wa_plane = sb.tile([P, 2 * R], U8, align_bytes=64)
        wc_plane = sb.tile([P, R], U8, align_bytes=64)
        xt_plane = sb.tile([P, 2 * T], U8, align_bytes=64)
        xq_plane = sb.tile([P, T], U8, align_bytes=64)
        wb_plane = sb.tile([P, N], U8, align_bytes=64)
        wd_plane = sb.tile([P, N], U8, align_bytes=64)
        HALF = T // 2
        xt_codes = [sb.tile([P, 2, HALF], U32, name="xt_codes%d" % h, align_bytes=64) for h in range(2)]
        xq_codes = [sb.tile([P, 1, HALF], U32, name="xq_codes%d" % h, align_bytes=64) for h in range(2)]
        ur_cols = sb.tile([P, PACK], F32)
        wb_codes = sb.tile([P, 1, N], U32, align_bytes=64)
        wd_codes = sb.tile([P, 1, 2 * N], U8, align_bytes=64)
        us_cols = sb.tile([P, PACK], F32)
        ur_row = sb.tile([1, R], F32)
        ur_slots = sb.tile([P, R], F32)
        ident = sb.tile([P, P], F32)

        nc.gpsimd.memset(xt_plane[:].bitcast(I32), 0)
        nc.vector.memset(wa_plane[:].bitcast(I32), 0)
        nc.vector.memset(xq_plane[:].bitcast(I32), 0)
        nc.vector.memset(wc_plane[:].bitcast(I32), 0)

        both = [nc.sync, nc.scalar]

        def load_words(queue, dst, words):
            if words.ndim == 4:
                words = words.rearrange("g p n t -> g p (n t)")
            queue.dma_start(out=dst[:].bitcast(I32), in_=words.rearrange("g p b -> p g b").bitcast(I32))

        def load_scales(queues, dst, scales, quadrants):
            passes = scales.shape[0]
            for q in quadrants:
                queues[q % len(queues)].dma_start(
                    out=dst[32 * q : 32 * q + 4, :].bitcast(I32).rearrange("r (g c) -> r g c", g=passes),
                    in_=scales[:, 4 * q : 4 * q + 4, :].rearrange("g r c -> r g c").bitcast(I32),
                )

        load_scales([nc.gpsimd], xt_plane, xt_scales, range(2))
        load_scales([nc.gpsimd], xq_plane, xq_scales, range(2))
        make_identity(nc, ident[:])

        swapped = [nc.scalar, nc.sync]
        load_words(nc.sync, wa_raw, wa_words)
        load_scales(swapped, wa_plane, wa_scales, range(4))
        load_scales(swapped, xt_plane, xt_scales, range(2, 4))
        load_words(nc.scalar, xt_codes[0], xt_words[:, :, 0:HALF, :])
        load_words(nc.sync, wc_raw, wc_words)
        load_words(nc.scalar, xq_codes[0], xq_words[:, :, 0:HALF, :])
        load_scales(both, wc_plane, wc_scales, range(4))
        load_scales(both, xq_plane, xq_scales, range(2, 4))
        nc.sync.dma_start(out=ur_row[:], in_=ur.rearrange("r o -> o r"))
        nc.sync.dma_start(out=us_cols[:], in_=us.rearrange("(p j) o -> p (j o)", j=PACK))
        load_words(nc.sync, xt_codes[1], xt_words[:, :, HALF:T, :])
        load_words(nc.sync, xq_codes[1], xq_words[:, :, HALF:T, :])
        load_words(nc.sync, wb_codes, wb_words)
        load_words(nc.sync, wd_codes, wd_words)

        w1_raw = [wa_raw[:, 0, :], wa_raw[:, 1, :], wc_raw[:, 0, :]]
        x_codes = [[xt_codes[h][:, 0, :], xt_codes[h][:, 1, :], xq_codes[h][:, 0, :]] for h in range(2)]
        x_planes = [xt_plane[:, 0:T], xt_plane[:, T : 2 * T], xq_plane[:]]
        w1_planes = [wa_plane[:, 0:R], wa_plane[:, R : 2 * R], wc_plane[:]]
        w2_planes = [wb_plane, wd_plane]
        w1_codes = []
        w1_scales = []
        for g in range(PASSES):
            codes = sb.tile([P, 2 * R], U8, align_bytes=64, name="w1_codes%d" % g)
            scales = sb.tile([P, R], U8, align_bytes=64, name="w1_scales%d" % g)
            nc.vector.tensor_copy(
                out=codes[:].bitcast(U16).rearrange("p (j m) -> p j m", j=PACK),
                in_=w1_raw[g].bitcast(U16).rearrange("p (m j) -> p j m", j=PACK),
            )
            nc.vector.tensor_copy(
                out=scales[:].rearrange("p (j m) -> p j m", j=PACK),
                in_=w1_planes[g].rearrange("p (m j) -> p j m", j=PACK),
            )
            w1_codes.append(codes)
            w1_scales.append(scales)

        nc.vector.memset(wb_plane[:].bitcast(I32), 0)
        nc.vector.memset(wd_plane[:].bitcast(I32), 0)
        load_scales([nc.sync], wb_plane, wb_scales, range(4))
        load_scales([nc.sync], wd_plane, wd_scales, range(4))

        nc.scalar.activation(
            out=ur_slots[:].rearrange("p (j m) -> p j m", j=PACK),
            in_=ident[:].unsqueeze(1).to_broadcast([P, PACK, P]),
            func=COPY,
            scale=0.0,
        )

        z = [ps.tile([P, PACK * TC], F32, name="z%d" % c, tag="bank", bufs=7) for c in range(CHUNKS)]
        ur_bank = ps.tile([P, PACK, P], F32)

        def first_layer(c, g):
            for j in range(PACK):
                nc.tensor.matmul_mx(
                    out=z[c][:, j * TC : (j + 1) * TC],
                    lhsT=w1_codes[g][:, 2 * P * j : 2 * P * (j + 1)].bitcast(FP4X4),
                    lhsT_scale=w1_scales[g][:, P * j : P * (j + 1)],
                    rhs=x_codes[c // 2][g][:, c % 2 * TC : (c % 2 + 1) * TC].bitcast(FP8X4),
                    rhs_scale=x_planes[g][:, c * TC : (c + 1) * TC],
                    start=(g == 0 and j == 0),
                    stop=(g == PASSES - 1 and j == PACK - 1),
                )

        def first_layer_chunk(c):
            for g in range(PASSES):
                first_layer(c, g)

        def spread_ur():
            nc.scalar.copy(
                out=ur_slots[0:1, :].rearrange("o (j p) -> o j p", j=PACK),
                in_=ur_row[:].rearrange("o (p j) -> o j p", j=PACK),
            )
            for j in range(PACK):
                nc.tensor.transpose(ur_bank[:, j, :], ur_slots[:, j * P : (j + 1) * P], ident[:])
            nc.scalar.copy(out=ur_cols[:], in_=ur_bank[:, :, 0])

        W = PACK * TC
        kept = [sb.tile([P, W], F32, name="kept%d" % c) for c in range(CHUNKS)]
        cut = [sb.tile([P, W], F32, name="cut%d" % c) for c in range(CHUNKS)]
        batches = [[(0, c), (1, c)] for c in range(CHUNKS - 1)] + [[(0, CHUNKS - 1)], [(1, CHUNKS - 1)]]
        hidden = {}
        h_codes = {}
        h_scales = {}
        batch_tiles = []
        for b, batch in enumerate(batches):
            values = sb.tile([P, len(batch) * W], BF16, name="hidden%d" % b, align_bytes=64)
            codes = sb.tile([P, len(batch) * TC], U32, name="h_codes%d" % b, align_bytes=64)
            scales = sb.tile([P, len(batch) * TC], U8, name="h_scales%d" % b, align_bytes=64)
            batch_tiles.append((values, codes, scales))
            for s, key in enumerate(batch):
                hidden[key] = values[:, s * W : (s + 1) * W]
                h_codes[key] = codes[:, s * TC : (s + 1) * TC]
                h_scales[key] = scales[:, s * TC : (s + 1) * TC]

        def by_token(ap):
            return ap.rearrange("p (t j) -> p t j", j=PACK)

        def z_by_token(c):
            return z[c][:].rearrange("p (j t) -> p t j", j=PACK)


        def keep(c, first):
            nc.vector.tensor_scalar(
                out=by_token(kept[c][:]), in0=z_by_token(c), scalar1=1.0, scalar2=-1.0, op0=ALU.min, op1=ALU.max
            )
            nc.gpsimd.tensor_tensor(
                out=by_token(hidden[0, c])[:, first:TC, :],
                in0=by_token(kept[c][:])[:, first:TC, :],
                in1=us_cols[:].unsqueeze(1).to_broadcast([P, TC - first, PACK]),
                op=ALU.mult,
            )

        def cut_off(c):
            nc.vector.tensor_tensor(out=by_token(cut[c][:]), in0=z_by_token(c), in1=by_token(kept[c][:]), op=ALU.subtract)

        def scale_cut(c, first):
            nc.vector.tensor_tensor(
                out=by_token(hidden[1, c])[:, first:TC, :],
                in0=by_token(cut[c][:])[:, first:TC, :],
                in1=ur_bank[:, :, 0].unsqueeze(1).to_broadcast([P, TC - first, PACK]),
                op=ALU.mult,
            )

        def scale_on_scalar(dst, src, factors):
            for j in range(PACK):
                nc.scalar.activation(
                    out=by_token(dst)[:, 0:SCALAR_TOKENS, j],
                    in_=by_token(src[:])[:, 0:SCALAR_TOKENS, j],
                    func=COPY,
                    scale=factors[:, j : j + 1],
                )

        def quantise(b):
            values, codes, scales = batch_tiles[b]
            nc.vector.quantize_mx(out=codes[:].bitcast(FP8X4), scales=scales[:], in_=values[:])

        out_v = out.rearrange("(i p) t -> p i t", p=P)

        def open_banks(c, groups):
            return [(ps.tile([P, len(g) * TC], F32, name="y%d_%d" % (c, g[0]), tag="bank", bufs=7), g) for g in groups]

        def second_layer(part, c, banks):
            for bank, tiles in banks:
                for s, i in enumerate(tiles):
                    if part == 0:
                        lhsT = wb_codes[:, 0, P * i : P * (i + 1)].bitcast(FP8X4)
                    else:
                        lhsT = wd_codes[:, 0, 2 * P * i : 2 * P * (i + 1)].bitcast(FP4X4)
                    nc.tensor.matmul_mx(
                        out=bank[:, s * TC : (s + 1) * TC],
                        lhsT=lhsT,
                        lhsT_scale=w2_planes[part][:, P * i : P * (i + 1)],
                        rhs=h_codes[part, c].bitcast(FP8X4),
                        rhs_scale=h_scales[part, c],
                        start=(part == 0 and s == 0),
                        stop=(part == 1 and s == len(tiles) - 1),
                    )

        def store(c, banks, queues):
            for b, (bank, tiles) in enumerate(banks):
                res = sb.tile([P, len(tiles) * TC], F32, name="res%d_%d" % (c, b))
                if b == 0:
                    nc.scalar.copy(out=res[:], in_=bank[:])
                else:
                    nc.vector.tensor_copy(out=res[:], in_=bank[:])
                queues[b].dma_start(
                    out=out_v[:, tiles[0] : tiles[-1] + 1, c * TC : (c + 1) * TC],
                    in_=res[:].rearrange("p (i t) -> p i t", t=TC),
                )

        def multiply(c):
            quantise(c)
            banks = open_banks(c, [[0, 1, 2, 3]])
            second_layer(0, c, banks)
            second_layer(1, c, banks)
            return banks

        first_layer(0, 0)
        first_layer(0, 1)
        first_layer(1, 0)
        first_layer(0, 2)
        first_layer(1, 1)
        first_layer(1, 2)
        keep(0, 0)
        spread_ur()
        first_layer_chunk(2)
        first_layer_chunk(3)
        cut_off(0)
        scale_on_scalar(hidden[1, 0], cut[0], ur_cols)
        keep(1, 0)
        scale_cut(0, SCALAR_TOKENS)
        cut_off(1)
        scale_on_scalar(hidden[1, 1], cut[1], ur_cols)
        keep(2, 0)
        store(0, multiply(0), [nc.sync])
        scale_cut(1, SCALAR_TOKENS)
        cut_off(2)
        keep(3, SCALAR_TOKENS)
        scale_on_scalar(hidden[0, 3], kept[3], us_cols)
        store(1, multiply(1), [nc.sync])
        scale_cut(2, 0)
        cut_off(3)
        store(2, multiply(2), [nc.sync])
        scale_cut(3, 0)
        quantise(3)
        quantise(4)
        banks = open_banks(3, [[0, 1], [2, 3]])
        second_layer(0, 3, banks)
        second_layer(1, 3, banks)
        store(3, banks, [nc.scalar, nc.sync])
